import numpy as np
import ml_dtypes


def mxq(x, axis, fmt="e4m3"):
    dtype, down = {"e4m3": (ml_dtypes.float8_e4m3fn, 7), "e5m2": (ml_dtypes.float8_e5m2, 14)}[fmt]
    v = np.moveaxis(np.asarray(x, np.float32).astype(ml_dtypes.bfloat16).astype(np.float64), axis, -1)
    blocks = v.reshape(v.shape[:-1] + (-1, 32))
    amax = np.abs(blocks).max(-1, keepdims=True)
    byte = np.maximum(np.where(amax > 0, np.frexp(amax)[1] - 1 + 127, 0) - down, 1)
    scale = np.exp2(byte - 127.0)
    codes = (blocks / scale).astype(np.float32).astype(dtype).astype(np.float64)
    return np.moveaxis((codes * scale).reshape(v.shape), -1, axis)


WIDE = False


def mx_kscale(k):
    if not WIDE:
        return np.ones(k)
    levels = np.array([10, -10, 5, -5, 0])
    if k % 512:
        return np.exp2(np.random.permutation(np.resize(levels, k // 32))).repeat(32)
    a = np.empty((k // 512, 16))
    for p in range(k // 512):
        a[p, :8] = np.random.permutation(np.resize(levels, 8))
        for g in range(8):
            far = levels[np.abs(levels - a[p, g]) >= 10]
            a[p, g + 8] = far[np.random.randint(len(far))]
    return np.exp2(a.ravel()).repeat(32)


def f64(x):
    return np.asarray(x).astype(np.float64)


def striped(idx):
    return np.tile(np.asarray(idx).reshape(-1, 16).T, (8, 1)).astype(np.uint16)


def unstriped(offs):
    return offs[:16].T.reshape(-1).astype(np.int64)


E2M1 = np.array([0.0, 0.5, 1.0, 1.5, 2.0, 3.0, 4.0, 6.0, -0.0, -0.5, -1.0, -1.5, -2.0, -3.0, -4.0, -6.0])


def pack_weight(w, fmt):
    k, n = w.shape
    w = f64(np.asarray(w, np.float32).astype(ml_dtypes.bfloat16)).reshape(k // 32, 32, n)
    amax = np.abs(w).max(1)
    if fmt == "e4m3":
        byte = np.frexp(amax)[1] - 1 + 127 - 7
    else:
        mant, ex = np.frexp(amax / 6.0)
        byte = np.where(mant > 0.5, ex, ex - 1) + 127
    byte = np.clip(np.where(amax > 0, byte, 1), 1, 254)
    scaled = (w * np.exp2(127.0 - byte)[:, None, :]).reshape(k, n).astype(np.float32)
    by_word = np.ascontiguousarray(scaled.reshape(k // 512, 128, 4, n).transpose(0, 1, 3, 2))
    if fmt == "e4m3":
        words = by_word.astype(ml_dtypes.float8_e4m3fn).view(np.uint8)
    else:
        c = by_word.astype(ml_dtypes.float4_e2m1fn).view(np.uint8) & 0xF
        words = (c[..., 0::2] | (c[..., 1::2] << 4)).reshape(k // 512, 128, 2 * n)
    return np.ascontiguousarray(words), np.ascontiguousarray(byte.astype(np.uint8).reshape(k // 512, 16, n))


def unpack_weight(words, scales, fmt):
    g, _, n = scales.shape
    words = np.ascontiguousarray(words).reshape(g, 128, n, -1)
    if fmt == "e4m3":
        vals = words.view(ml_dtypes.float8_e4m3fn).astype(np.float64)
    else:
        nib = np.empty((g, 128, n, 4), np.uint8)
        nib[..., 0::2] = words & 0xF
        nib[..., 1::2] = words >> 4
        vals = E2M1[nib]
    vals = vals * np.repeat(np.exp2(scales.astype(np.float64) - 127.0), 8, axis=1)[..., None]
    return vals.transpose(0, 1, 3, 2).reshape(g * 512, n)


K, T, J, R, N = 1024, 1024, 384, 512, 256


def setup_inputs():
    n = np.random.standard_normal
    idx = np.random.permutation(T)[:J]
    fk = mx_kscale(K)
    fr = mx_kscale(R)
    wp = pack_weight(n((K, R)) * 1 / np.sqrt(K) * fk[:, None] * fr, "e2m1")
    wbp = pack_weight(n((R, N)) * 1 / np.sqrt(R) / fr[:, None], "e2m1")
    return {
        "xf": (n((K, T))).astype(np.float32),
        "ow": (n((K, J)) * 0.7).astype(np.float32),
        "fk": (np.random.uniform(0.5, 2.0, (K, 1)) / fk[:, None]).astype(np.float32),
        "w_words": wp[0],
        "w_scales": wp[1],
        "wb_words": wbp[0],
        "wb_scales": wbp[1],
        "rs": (1.0 * n((J, N))).astype(np.float32),
        "offs": striped(idx),
    }


def reference(xf, ow, fk, w_words, w_scales, wb_words, wb_scales, rs, offs):
    idx = unstriped(offs)
    wu = unpack_weight(w_words, w_scales, "e2m1")
    wbu = unpack_weight(wb_words, wb_scales, "e2m1")
    u = (f64(xf)[:, idx] - f64(ow)) * f64(fk)
    uq = mxq(u, 0, "e4m3")
    a = wu.T @ uq
    hid = np.maximum(a, 0.0)
    hidq = mxq(hid, 0, "e4m3")
    p = hidq.T @ wbu
    pk2 = np.max(np.abs(p), axis=1, keepdims=True)
    y = p / (pk2 + 0.2) + 0.3 * f64(rs)
    return y

@@ -1,0 +1,168 @@
+from contextlib import ExitStack
+
+import concourse.mybir as mybir
+
+K, T, J, R, N = 1024, 1024, 384, 512, 256
+FLOPS = 2 * K * R * J + 2 * R * N * J
+
+F32 = mybir.dt.float32
+BF16 = mybir.dt.bfloat16
+I32 = mybir.dt.int32
+U32 = mybir.dt.uint32
+U16 = mybir.dt.uint16
+U8 = mybir.dt.uint8
+FP8X4 = mybir.dt.float8_e4m3fn_x4
+FP4X4 = mybir.dt.float4_e2m1fn_x4
+ALU = mybir.AluOpType
+ACT = mybir.ActivationFunctionType
+
+P = 128
+PACK = 4
+PASSES = K // (P * PACK)
+SLICES = J // P
+LIST_COLS = P // 16
+
+
+def tile_list_offsetpicks_plain_rowpeaks_kernel(tc, xf, ow, fk, w_words, w_scales, wb_words, wb_scales, rs, offs, out):
+    nc = tc.nc
+    with ExitStack() as ctx:
+        keep = ctx.enter_context(tc.tile_pool(name="keep", bufs=1))
+        ring = ctx.enter_context(tc.tile_pool(name="ring", bufs=3))
+        psum = ctx.enter_context(tc.psum_pool(name="psum", bufs=1))
+
+        offsets = keep.tile([P, J // 16], U16, name="offsets")
+        nc.sync.dma_start(offsets[:], offs)
+
+        ws_raw = keep.tile([P, PASSES, R], U8, name="ws_raw", align_bytes=64)
+        wb_sc = keep.tile([P, N], U8, name="wb_sc", align_bytes=64)
+        nc.vector.memset(ws_raw[:].rearrange("p a n -> p (a n)").bitcast(I32), 0)
+        nc.vector.memset(wb_sc[:].bitcast(I32), 0)
+
+        x_rows = xf.rearrange("(a p t) n -> a t p n", a=PASSES, t=PACK)
+        ow_rows = ow.rearrange("(a p t) j -> a p t j", a=PASSES, t=PACK)
+        x_sb = [[keep.tile([P, T], F32, name="x%d%d" % (a, t)) for t in range(PACK)] for a in range(PASSES)]
+        ow_first = keep.tile([P, J], F32, name="ow_first")
+        ow_rest = keep.tile([P, PACK - 1, J], F32, name="ow_rest")
+        ow_lead = keep.tile([P, PACK - 1, J], F32, name="ow_lead")
+        ow_last = keep.tile([P, J], F32, name="ow_last")
+        ow_sb = [
+            [ow_first[:]] + [ow_rest[:, t, :] for t in range(PACK - 1)],
+            [ow_lead[:, t, :] for t in range(PACK - 1)] + [ow_last[:]],
+        ]
+        fk_sb = keep.tile([P, PASSES, PACK], F32, name="fk_sb")
+        w_raw = keep.tile([P, PASSES, 2 * R], U8, name="w_raw", align_bytes=64)
+        wb_sb = keep.tile([P, 2 * N], U8, name="wb_sb", align_bytes=64)
+        rs_sb = keep.tile([P, SLICES, N], F32, name="rs_sb")
+
+        nc.sync.dma_start(ow_first[:], ow_rows[0][:, 0, :])
+        nc.sync.dma_start(x_sb[0][0][:], x_rows[0, 0])
+        nc.sync.dma_start(fk_sb[:], fk.rearrange("(a p t) o -> p a (t o)", a=PASSES, t=PACK))
+        nc.sync.dma_start(w_raw[:].bitcast(I32), w_words.rearrange("a p n -> p a n").bitcast(I32))
+        nc.sync.dma_start(ow_rest[:], ow_rows[0][:, 1:, :])
+        nc.sync.dma_start(x_sb[0][1][:], x_rows[0, 1])
+        nc.sync.dma_start(x_sb[0][2][:], x_rows[0, 2])
+        for q in range(4):
+            nc.sync.dma_start(
+                ws_raw[32 * q : 32 * q + 4].bitcast(I32),
+                w_scales[:, 4 * q : 4 * q + 4, :].rearrange("a r n -> r a n").bitcast(I32),
+            )
+        nc.sync.dma_start(x_sb[0][3][:], x_rows[0, 3])
+        nc.sync.dma_start(ow_lead[:], ow_rows[1][:, : PACK - 1, :])
+        for t in range(PACK - 1):
+            nc.sync.dma_start(x_sb[1][t][:], x_rows[1, t])
+        nc.sync.dma_start(ow_last[:], ow_rows[1][:, PACK - 1, :])
+        nc.sync.dma_start(x_sb[1][PACK - 1][:], x_rows[1, PACK - 1])
+        nc.sync.dma_start(wb_sb[:].bitcast(I32), wb_words[0].bitcast(I32))
+        for q in range(4):
+            nc.sync.dma_start(wb_sc[32 * q : 32 * q + 4].bitcast(I32), wb_scales[0, 4 * q : 4 * q + 4, :].bitcast(I32))
+        nc.sync.dma_start(rs_sb[:], rs.rearrange("(s p) n -> p s n", p=P))
+
+        w_perm = keep.tile([P, PASSES, 2 * R], U8, name="w_perm", align_bytes=64)
+        ws_perm = keep.tile([P, PASSES, R], U8, name="ws_perm", align_bytes=64)
+
+        acc = [psum.tile([P, PACK, P], F32, name="acc%d" % s) for s in range(SLICES)]
+        prod = [psum.tile([P, N], F32, name="prod%d" % s) for s in range(SLICES)]
+        u_bf = [keep.tile([P, J, PACK], BF16, name="u%d" % a, align_bytes=64) for a in range(PASSES)]
+        u_codes = [keep.tile([P, J], U32, name="uc%d" % a, align_bytes=64) for a in range(PASSES)]
+        u_sc = [keep.tile([P, J], U8, name="us%d" % a, align_bytes=64) for a in range(PASSES)]
+
+        def plane(a, t, lo, hi):
+            diff = ring.tile([P, hi - lo], F32, name="diff", bufs=6)
+            picks = offsets[:, lo // 16 : hi // 16]
+            nc.vector.tensor_tensor(diff[:], x_sb[a][t][:].indirect(picks), ow_sb[a][t][:, lo:hi], ALU.subtract)
+            return diff
+
+        def scale_round(a, t, lo, hi, diff, on_vector=False):
+            if on_vector:
+                nc.vector.tensor_scalar(u_bf[a][:, lo:hi, t], diff[:], fk_sb[:, a, t : t + 1], None, ALU.mult)
+            else:
+                nc.scalar.activation(u_bf[a][:, lo:hi, t], diff[:], ACT.Copy, scale=fk_sb[:, a, t : t + 1])
+
+        def quantise_u(a, lo, hi):
+            nc.vector.quantize_mx(u_codes[a][:, lo:hi].bitcast(FP8X4), u_sc[a][:, lo:hi], u_bf[a][:, lo:hi, :].rearrange("p j t -> p (j t)"))
+
+        def first_product(a, s):
+            cols = slice(s * P, (s + 1) * P)
+            for t in range(PACK):
+                nc.tensor.matmul_mx(
+                    acc[s][:, t, :],
+                    lhsT=w_perm[:, a, 2 * P * t : 2 * P * (t + 1)].bitcast(FP4X4),
+                    lhsT_scale=ws_perm[:, a, P * t : P * (t + 1)],
+                    rhs=u_codes[a][:, cols].bitcast(FP8X4),
+                    rhs_scale=u_sc[a][:, cols],
+                    start=(a == 0 and t == 0),
+                    stop=(a == PASSES - 1 and t == PACK - 1),
+                )
+
+        scale_round(0, 0, 0, J, plane(0, 0, 0, J))
+        for a in range(PASSES):
+            nc.vector.tensor_copy(
+                w_perm[:, a, :].bitcast(U16).rearrange("p (t m) -> p t m", t=PACK),
+                w_raw[:, a, :].bitcast(U16).rearrange("p (m t) -> p t m", t=PACK),
+            )
+        for t in (1, 2):
+            scale_round(0, t, 0, J, plane(0, t, 0, J))
+        for a in range(PASSES):
+            nc.vector.tensor_copy(
+                ws_perm[:, a, :].rearrange("p (t m) -> p t m", t=PACK),
+                ws_raw[:, a, :].rearrange("p (m t) -> p t m", t=PACK),
+            )
+        scale_round(0, 3, 0, J, plane(0, 3, 0, J))
+        quantise_u(0, 0, J)
+        for s in range(SLICES):
+            first_product(0, s)
+        for t in range(PACK):
+            for s in range(SLICES):
+                scale_round(1, t, s * P, (s + 1) * P, plane(1, t, s * P, (s + 1) * P))
+        for s in range(SLICES):
+            quantise_u(1, s * P, (s + 1) * P)
+            first_product(1, s)
+
+        rs3 = keep.tile([P, SLICES, N], F32, name="rs3")
+        nc.vector.tensor_scalar(rs3[:], rs_sb[:], 0.3, None, ALU.mult)
+
+        for s in range(SLICES):
+            hid = ring.tile([P, P, PACK], BF16, name="hid", align_bytes=64)
+            nc.scalar.activation(hid[:], acc[s][:].rearrange("p t j -> p j t"), ACT.Relu)
+            h_codes = ring.tile([P, P], U32, name="h_codes", align_bytes=64)
+            h_sc = ring.tile([P, P], U8, name="h_sc", align_bytes=64)
+            nc.vector.quantize_mx(h_codes[:].bitcast(FP8X4), h_sc[:], hid[:].rearrange("p j t -> p (j t)"))
+            nc.tensor.matmul_mx(
+                prod[s][:],
+                lhsT=h_codes[:].bitcast(FP8X4),
+                lhsT_scale=h_sc[:],
+                rhs=wb_sb[:].bitcast(FP4X4),
+                rhs_scale=wb_sc[:],
+                start=True,
+                stop=True,
+            )
+        for s in range(SLICES):
+            mag = ring.tile([P, N], F32, name="mag")
+            nc.scalar.activation(mag[:], prod[s][:], ACT.Abs)
+            den = ring.tile([P, 1], F32, name="den")
+            nc.vector.tensor_scalar(mag[:], mag[:], 0.2, None, ALU.add, ALU.max, accum_out=den[:])
+            inv = ring.tile([P, 1], F32, name="inv")
+            nc.vector.reciprocal(inv[:], den[:])
+            res = ring.tile([P, N], F32, name="res")
+            nc.vector.scalar_tensor_tensor(res[:], prod[s][:], inv[:], rs3[:, s, :], ALU.mult, ALU.add)
+            nc.sync.dma_start(out[s * P : (s + 1) * P, :], res[:])

@@ -20,7 +20,7 @@ P = 128
 PACK = 4
 PASSES = K // (P * PACK)
 SLICES = J // P
-LIST_COLS = P // 16
+ORDER = (0, 1, 2, 3)
 
 
 def tile_list_offsetpicks_plain_rowpeaks_kernel(tc, xf, ow, fk, w_words, w_scales, wb_words, wb_scales, rs, offs, out):
@@ -31,65 +31,70 @@ def tile_list_offsetpicks_plain_rowpeaks_kernel(tc, xf, ow, fk, w_words, w_scale
         psum = ctx.enter_context(tc.psum_pool(name="psum", bufs=1))
 
         offsets = keep.tile([P, J // 16], U16, name="offsets")
-        nc.sync.dma_start(offsets[:], offs)
 
         ws_raw = keep.tile([P, PASSES, R], U8, name="ws_raw", align_bytes=64)
         wb_sc = keep.tile([P, N], U8, name="wb_sc", align_bytes=64)
-        nc.vector.memset(ws_raw[:].rearrange("p a n -> p (a n)").bitcast(I32), 0)
+        nc.gpsimd.memset(ws_raw[:].rearrange("p a n -> p (a n)").bitcast(I32), 0)
         nc.vector.memset(wb_sc[:].bitcast(I32), 0)
 
         x_rows = xf.rearrange("(a p t) n -> a t p n", a=PASSES, t=PACK)
         ow_rows = ow.rearrange("(a p t) j -> a p t j", a=PASSES, t=PACK)
         x_sb = [[keep.tile([P, T], F32, name="x%d%d" % (a, t)) for t in range(PACK)] for a in range(PASSES)]
-        ow_first = keep.tile([P, J], F32, name="ow_first")
-        ow_rest = keep.tile([P, PACK - 1, J], F32, name="ow_rest")
-        ow_lead = keep.tile([P, PACK - 1, J], F32, name="ow_lead")
-        ow_last = keep.tile([P, J], F32, name="ow_last")
-        ow_sb = [
-            [ow_first[:]] + [ow_rest[:, t, :] for t in range(PACK - 1)],
-            [ow_lead[:, t, :] for t in range(PACK - 1)] + [ow_last[:]],
-        ]
+        ow_pair = [keep.tile([P, 2, J], F32, name="ow0%d" % h) for h in range(2)]
+        ow_one = [keep.tile([P, J], F32, name="ow1%d" % t, tag="ow1%d" % t, align_bytes=64) for t in range(PACK - 1)]
+        ow_head = keep.tile([P, P], F32, name="ow_head")
+        ow_tail = keep.tile([P, J - P], F32, name="ow_tail")
+
+        def centres(a, t, s):
+            if a == 0:
+                return ow_pair[t // 2][:, t % 2, s * P : (s + 1) * P]
+            if t < PACK - 1:
+                return ow_one[t][:, s * P : (s + 1) * P]
+            return ow_head[:] if s == 0 else ow_tail[:, (s - 1) * P : s * P]
+
         fk_sb = keep.tile([P, PASSES, PACK], F32, name="fk_sb")
-        w_raw = keep.tile([P, PASSES, 2 * R], U8, name="w_raw", align_bytes=64)
+        w_raw = [keep.tile([P, 2 * R], U8, name="w_raw%d" % a, align_bytes=64) for a in range(PASSES)]
         wb_sb = keep.tile([P, 2 * N], U8, name="wb_sb", align_bytes=64)
         rs_sb = keep.tile([P, SLICES, N], F32, name="rs_sb")
 
-        nc.sync.dma_start(ow_first[:], ow_rows[0][:, 0, :])
-        nc.sync.dma_start(x_sb[0][0][:], x_rows[0, 0])
+        nc.sync.dma_start(w_raw[0][:].bitcast(I32), w_words[0].bitcast(I32))
+        nc.sync.dma_start(offsets[:], offs)
         nc.sync.dma_start(fk_sb[:], fk.rearrange("(a p t) o -> p a (t o)", a=PASSES, t=PACK))
-        nc.sync.dma_start(w_raw[:].bitcast(I32), w_words.rearrange("a p n -> p a n").bitcast(I32))
-        nc.sync.dma_start(ow_rest[:], ow_rows[0][:, 1:, :])
-        nc.sync.dma_start(x_sb[0][1][:], x_rows[0, 1])
-        nc.sync.dma_start(x_sb[0][2][:], x_rows[0, 2])
-        for q in range(4):
-            nc.sync.dma_start(
-                ws_raw[32 * q : 32 * q + 4].bitcast(I32),
-                w_scales[:, 4 * q : 4 * q + 4, :].rearrange("a r n -> r a n").bitcast(I32),
-            )
-        nc.sync.dma_start(x_sb[0][3][:], x_rows[0, 3])
-        nc.sync.dma_start(ow_lead[:], ow_rows[1][:, : PACK - 1, :])
-        for t in range(PACK - 1):
-            nc.sync.dma_start(x_sb[1][t][:], x_rows[1, t])
-        nc.sync.dma_start(ow_last[:], ow_rows[1][:, PACK - 1, :])
-        nc.sync.dma_start(x_sb[1][PACK - 1][:], x_rows[1, PACK - 1])
+        for a in range(PASSES):
+            for t in ORDER:
+                if a == 1 and t == PACK - 1:
+                    nc.sync.dma_start(ow_head[:], ow_rows[a][:, t, :P])
+                elif a == 1:
+                    nc.sync.dma_start(ow_one[t][:], ow_rows[a][:, t, :])
+                elif t % 2 == 0:
+                    nc.sync.dma_start(ow_pair[t // 2][:], ow_rows[a][:, t : t + 2, :])
+                nc.sync.dma_start(x_sb[a][t][:], x_rows[a, t])
+                if a == 0 and t == ORDER[0]:
+                    for q in range(4):
+                        nc.sync.dma_start(
+                            ws_raw[32 * q : 32 * q + 4].bitcast(I32),
+                            w_scales[:, 4 * q : 4 * q + 4, :].rearrange("a r n -> r a n").bitcast(I32),
+                        )
+        nc.sync.dma_start(ow_tail[:], ow_rows[1][:, PACK - 1, P:])
+        nc.sync.dma_start(w_raw[1][:].bitcast(I32), w_words[1].bitcast(I32))
+        nc.sync.dma_start(rs_sb[:], rs.rearrange("(s p) n -> p s n", p=P))
         nc.sync.dma_start(wb_sb[:].bitcast(I32), wb_words[0].bitcast(I32))
         for q in range(4):
             nc.sync.dma_start(wb_sc[32 * q : 32 * q + 4].bitcast(I32), wb_scales[0, 4 * q : 4 * q + 4, :].bitcast(I32))
-        nc.sync.dma_start(rs_sb[:], rs.rearrange("(s p) n -> p s n", p=P))
 
-        w_perm = keep.tile([P, PASSES, 2 * R], U8, name="w_perm", align_bytes=64)
+        w_perm = [keep.tile([P, 2 * R], U8, name="w_perm%d" % a, align_bytes=64) for a in range(PASSES)]
         ws_perm = keep.tile([P, PASSES, R], U8, name="ws_perm", align_bytes=64)
 
         acc = [psum.tile([P, PACK, P], F32, name="acc%d" % s) for s in range(SLICES)]
         prod = [psum.tile([P, N], F32, name="prod%d" % s) for s in range(SLICES)]
         u_bf = [keep.tile([P, J, PACK], BF16, name="u%d" % a, align_bytes=64) for a in range(PASSES)]
-        u_codes = [keep.tile([P, J], U32, name="uc%d" % a, align_bytes=64) for a in range(PASSES)]
+        u_codes = [keep.tile([P, J], U32, name="uc%d" % a, tag=("ow11", "uc1")[a], align_bytes=64) for a in range(PASSES)]
         u_sc = [keep.tile([P, J], U8, name="us%d" % a, align_bytes=64) for a in range(PASSES)]
 
         def plane(a, t, lo, hi):
             diff = ring.tile([P, hi - lo], F32, name="diff", bufs=6)
             picks = offsets[:, lo // 16 : hi // 16]
-            nc.vector.tensor_tensor(diff[:], x_sb[a][t][:].indirect(picks), ow_sb[a][t][:, lo:hi], ALU.subtract)
+            nc.vector.tensor_tensor(diff[:], x_sb[a][t][:].indirect(picks), centres(a, t, lo // P), ALU.subtract)
             return diff
 
         def scale_round(a, t, lo, hi, diff, on_vector=False):
@@ -106,7 +111,7 @@ def tile_list_offsetpicks_plain_rowpeaks_kernel(tc, xf, ow, fk, w_words, w_scale
             for t in range(PACK):
                 nc.tensor.matmul_mx(
                     acc[s][:, t, :],
-                    lhsT=w_perm[:, a, 2 * P * t : 2 * P * (t + 1)].bitcast(FP4X4),
+                    lhsT=w_perm[a][:, 2 * P * t : 2 * P * (t + 1)].bitcast(FP4X4),
                     lhsT_scale=ws_perm[:, a, P * t : P * (t + 1)],
                     rhs=u_codes[a][:, cols].bitcast(FP8X4),
                     rhs_scale=u_sc[a][:, cols],
@@ -114,26 +119,27 @@ def tile_list_offsetpicks_plain_rowpeaks_kernel(tc, xf, ow, fk, w_words, w_scale
                     stop=(a == PASSES - 1 and t == PACK - 1),
                 )
 
-        scale_round(0, 0, 0, J, plane(0, 0, 0, J))
-        for a in range(PASSES):
+        def deal_words(a):
             nc.vector.tensor_copy(
-                w_perm[:, a, :].bitcast(U16).rearrange("p (t m) -> p t m", t=PACK),
-                w_raw[:, a, :].bitcast(U16).rearrange("p (m t) -> p t m", t=PACK),
+                w_perm[a][:].bitcast(U16).rearrange("p (t m) -> p t m", t=PACK),
+                w_raw[a][:].bitcast(U16).rearrange("p (m t) -> p t m", t=PACK),
             )
-        for t in (1, 2):
-            scale_round(0, t, 0, J, plane(0, t, 0, J))
+
+        deal_words(0)
         for a in range(PASSES):
-            nc.vector.tensor_copy(
-                ws_perm[:, a, :].rearrange("p (t m) -> p t m", t=PACK),
-                ws_raw[:, a, :].rearrange("p (m t) -> p t m", t=PACK),
-            )
-        scale_round(0, 3, 0, J, plane(0, 3, 0, J))
-        quantise_u(0, 0, J)
-        for s in range(SLICES):
-            first_product(0, s)
-        for t in range(PACK):
-            for s in range(SLICES):
-                scale_round(1, t, s * P, (s + 1) * P, plane(1, t, s * P, (s + 1) * P))
+            for t in range(PACK):
+                for s in range(SLICES):
+                    scale_round(a, t, s * P, (s + 1) * P, plane(a, t, s * P, (s + 1) * P))
+                if a == 0 and t in (1, 2):
+                    nc.vector.tensor_copy(
+                        ws_perm[:, t - 1, :].rearrange("p (t m) -> p t m", t=PACK),
+                        ws_raw[:, t - 1, :].rearrange("p (m t) -> p t m", t=PACK),
+                    )
+                if a == 1 and t == 1:
+                    quantise_u(0, 0, J)
+                    for s in range(SLICES):
+                        first_product(0, s)
+        deal_words(1)
         for s in range(SLICES):
             quantise_u(1, s * P, (s + 1) * P)
             first_product(1, s)
@@ -141,9 +147,12 @@ def tile_list_offsetpicks_plain_rowpeaks_kernel(tc, xf, ow, fk, w_words, w_scale
         rs3 = keep.tile([P, SLICES, N], F32, name="rs3")
         nc.vector.tensor_scalar(rs3[:], rs_sb[:], 0.3, None, ALU.mult)
 
-        for s in range(SLICES):
+        def second_product(s):
             hid = ring.tile([P, P, PACK], BF16, name="hid", align_bytes=64)
-            nc.scalar.activation(hid[:], acc[s][:].rearrange("p t j -> p j t"), ACT.Relu)
+            if s == 1:
+                nc.vector.tensor_scalar(hid[:], acc[s][:].rearrange("p t j -> p j t"), 0.0, None, ALU.max)
+            else:
+                nc.scalar.activation(hid[:], acc[s][:].rearrange("p t j -> p j t"), ACT.Relu)
             h_codes = ring.tile([P, P], U32, name="h_codes", align_bytes=64)
             h_sc = ring.tile([P, P], U8, name="h_sc", align_bytes=64)
             nc.vector.quantize_mx(h_codes[:].bitcast(FP8X4), h_sc[:], hid[:].rearrange("p j t -> p (j t)"))
@@ -156,13 +165,27 @@ def tile_list_offsetpicks_plain_rowpeaks_kernel(tc, xf, ow, fk, w_words, w_scale
                 start=True,
                 stop=True,
             )
-        for s in range(SLICES):
+
+        def peak(s):
             mag = ring.tile([P, N], F32, name="mag")
             nc.scalar.activation(mag[:], prod[s][:], ACT.Abs)
             den = ring.tile([P, 1], F32, name="den")
             nc.vector.tensor_scalar(mag[:], mag[:], 0.2, None, ALU.add, ALU.max, accum_out=den[:])
+            return den
+
+        def invert(den):
             inv = ring.tile([P, 1], F32, name="inv")
             nc.vector.reciprocal(inv[:], den[:])
+            return inv
+
+        def finish(s, inv):
             res = ring.tile([P, N], F32, name="res")
             nc.vector.scalar_tensor_tensor(res[:], prod[s][:], inv[:], rs3[:, s, :], ALU.mult, ALU.add)
             nc.sync.dma_start(out[s * P : (s + 1) * P, :], res[:])
+
+        for s in range(SLICES):
+            second_product(s)
+        dens = [peak(s) for s in range(SLICES)]
+        invs = [invert(den) for den in dens]
+        for s in range(SLICES):
+            finish(s, invs[s])

from contextlib import ExitStack

import concourse.mybir as mybir

K, T, J, R, N = 1024, 1024, 384, 512, 256
FLOPS = 2 * K * R * J + 2 * R * N * J

F32 = mybir.dt.float32
BF16 = mybir.dt.bfloat16
I32 = mybir.dt.int32
U32 = mybir.dt.uint32
U16 = mybir.dt.uint16
U8 = mybir.dt.uint8
FP8X4 = mybir.dt.float8_e4m3fn_x4
FP4X4 = mybir.dt.float4_e2m1fn_x4
ALU = mybir.AluOpType
ACT = mybir.ActivationFunctionType

P = 128
PACK = 4
PASSES = K // (P * PACK)
SLICES = J // P
ORDER = (0, 1, 2, 3)


def tile_list_offsetpicks_plain_rowpeaks_kernel(tc, xf, ow, fk, w_words, w_scales, wb_words, wb_scales, rs, offs, out):
    nc = tc.nc
    with ExitStack() as ctx:
        keep = ctx.enter_context(tc.tile_pool(name="keep", bufs=1))
        ring = ctx.enter_context(tc.tile_pool(name="ring", bufs=3))
        psum = ctx.enter_context(tc.psum_pool(name="psum", bufs=1))

        offsets = keep.tile([P, J // 16], U16, name="offsets")

        ws_raw = keep.tile([P, PASSES, R], U8, name="ws_raw", align_bytes=64)
        wb_sc = keep.tile([P, N], U8, name="wb_sc", align_bytes=64)
        nc.gpsimd.memset(ws_raw[:].rearrange("p a n -> p (a n)").bitcast(I32), 0)
        nc.vector.memset(wb_sc[:].bitcast(I32), 0)

        x_rows = xf.rearrange("(a p t) n -> a t p n", a=PASSES, t=PACK)
        ow_rows = ow.rearrange("(a p t) j -> a p t j", a=PASSES, t=PACK)
        x_sb = [[keep.tile([P, T], F32, name="x%d%d" % (a, t)) for t in range(PACK)] for a in range(PASSES)]
        ow_pair = [keep.tile([P, 2, J], F32, name="ow0%d" % h) for h in range(2)]
        ow_one = [keep.tile([P, J], F32, name="ow1%d" % t, tag="ow1%d" % t, align_bytes=64) for t in range(PACK - 1)]
        ow_head = keep.tile([P, P], F32, name="ow_head")
        ow_tail = keep.tile([P, J - P], F32, name="ow_tail")

        def centres(a, t, s):
            if a == 0:
                return ow_pair[t // 2][:, t % 2, s * P : (s + 1) * P]
            if t < PACK - 1:
                return ow_one[t][:, s * P : (s + 1) * P]
            return ow_head[:] if s == 0 else ow_tail[:, (s - 1) * P : s * P]

        fk_sb = keep.tile([P, PASSES, PACK], F32, name="fk_sb")
        w_raw = [keep.tile([P, 2 * R], U8, name="w_raw%d" % a, align_bytes=64) for a in range(PASSES)]
        wb_sb = keep.tile([P, 2 * N], U8, name="wb_sb", align_bytes=64)
        rs_sb = keep.tile([P, SLICES, N], F32, name="rs_sb")

        nc.sync.dma_start(w_raw[0][:].bitcast(I32), w_words[0].bitcast(I32))
        nc.sync.dma_start(offsets[:], offs)
        nc.sync.dma_start(fk_sb[:], fk.rearrange("(a p t) o -> p a (t o)", a=PASSES, t=PACK))
        for a in range(PASSES):
            for t in ORDER:
                if a == 1 and t == PACK - 1:
                    nc.sync.dma_start(ow_head[:], ow_rows[a][:, t, :P])
                elif a == 1:
                    nc.sync.dma_start(ow_one[t][:], ow_rows[a][:, t, :])
                elif t % 2 == 0:
                    nc.sync.dma_start(ow_pair[t // 2][:], ow_rows[a][:, t : t + 2, :])
                nc.sync.dma_start(x_sb[a][t][:], x_rows[a, t])
                if a == 0 and t == ORDER[0]:
                    for q in range(4):
                        nc.sync.dma_start(
                            ws_raw[32 * q : 32 * q + 4].bitcast(I32),
                            w_scales[:, 4 * q : 4 * q + 4, :].rearrange("a r n -> r a n").bitcast(I32),
                        )
        nc.sync.dma_start(ow_tail[:], ow_rows[1][:, PACK - 1, P:])
        nc.sync.dma_start(w_raw[1][:].bitcast(I32), w_words[1].bitcast(I32))
        nc.sync.dma_start(rs_sb[:], rs.rearrange("(s p) n -> p s n", p=P))
        nc.sync.dma_start(wb_sb[:].bitcast(I32), wb_words[0].bitcast(I32))
        for q in range(4):
            nc.sync.dma_start(wb_sc[32 * q : 32 * q + 4].bitcast(I32), wb_scales[0, 4 * q : 4 * q + 4, :].bitcast(I32))

        w_perm = [keep.tile([P, 2 * R], U8, name="w_perm%d" % a, align_bytes=64) for a in range(PASSES)]
        ws_perm = keep.tile([P, PASSES, R], U8, name="ws_perm", align_bytes=64)

        acc = [psum.tile([P, PACK, P], F32, name="acc%d" % s) for s in range(SLICES)]
        prod = [psum.tile([P, N], F32, name="prod%d" % s) for s in range(SLICES)]
        u_bf = [keep.tile([P, J, PACK], BF16, name="u%d" % a, align_bytes=64) for a in range(PASSES)]
        u_codes = [keep.tile([P, J], U32, name="uc%d" % a, tag=("ow11", "uc1")[a], align_bytes=64) for a in range(PASSES)]
        u_sc = [keep.tile([P, J], U8, name="us%d" % a, align_bytes=64) for a in range(PASSES)]

        def plane(a, t, lo, hi):
            diff = ring.tile([P, hi - lo], F32, name="diff", bufs=6)
            picks = offsets[:, lo // 16 : hi // 16]
            nc.vector.tensor_tensor(diff[:], x_sb[a][t][:].indirect(picks), centres(a, t, lo // P), ALU.subtract)
            return diff

        def scale_round(a, t, lo, hi, diff, on_vector=False):
            if on_vector:
                nc.vector.tensor_scalar(u_bf[a][:, lo:hi, t], diff[:], fk_sb[:, a, t : t + 1], None, ALU.mult)
            else:
                nc.scalar.activation(u_bf[a][:, lo:hi, t], diff[:], ACT.Copy, scale=fk_sb[:, a, t : t + 1])

        def quantise_u(a, lo, hi):
            nc.vector.quantize_mx(u_codes[a][:, lo:hi].bitcast(FP8X4), u_sc[a][:, lo:hi], u_bf[a][:, lo:hi, :].rearrange("p j t -> p (j t)"))

        def first_product(a, s):
            cols = slice(s * P, (s + 1) * P)
            for t in range(PACK):
                nc.tensor.matmul_mx(
                    acc[s][:, t, :],
                    lhsT=w_perm[a][:, 2 * P * t : 2 * P * (t + 1)].bitcast(FP4X4),
                    lhsT_scale=ws_perm[:, a, P * t : P * (t + 1)],
                    rhs=u_codes[a][:, cols].bitcast(FP8X4),
                    rhs_scale=u_sc[a][:, cols],
                    start=(a == 0 and t == 0),
                    stop=(a == PASSES - 1 and t == PACK - 1),
                )

        def deal_words(a):
            nc.vector.tensor_copy(
                w_perm[a][:].bitcast(U16).rearrange("p (t m) -> p t m", t=PACK),
                w_raw[a][:].bitcast(U16).rearrange("p (m t) -> p t m", t=PACK),
            )

        deal_words(0)
        for a in range(PASSES):
            for t in range(PACK):
                for s in range(SLICES):
                    scale_round(a, t, s * P, (s + 1) * P, plane(a, t, s * P, (s + 1) * P))
                if a == 0 and t in (1, 2):
                    nc.vector.tensor_copy(
                        ws_perm[:, t - 1, :].rearrange("p (t m) -> p t m", t=PACK),
                        ws_raw[:, t - 1, :].rearrange("p (m t) -> p t m", t=PACK),
                    )
                if a == 1 and t == 1:
                    quantise_u(0, 0, J)
                    for s in range(SLICES):
                        first_product(0, s)
        deal_words(1)
        for s in range(SLICES):
            quantise_u(1, s * P, (s + 1) * P)
            first_product(1, s)

        rs3 = keep.tile([P, SLICES, N], F32, name="rs3")
        nc.vector.tensor_scalar(rs3[:], rs_sb[:], 0.3, None, ALU.mult)

        def second_product(s):
            hid = ring.tile([P, P, PACK], BF16, name="hid", align_bytes=64)
            if s == 1:
                nc.vector.tensor_scalar(hid[:], acc[s][:].rearrange("p t j -> p j t"), 0.0, None, ALU.max)
            else:
                nc.scalar.activation(hid[:], acc[s][:].rearrange("p t j -> p j t"), ACT.Relu)
            h_codes = ring.tile([P, P], U32, name="h_codes", align_bytes=64)
            h_sc = ring.tile([P, P], U8, name="h_sc", align_bytes=64)
            nc.vector.quantize_mx(h_codes[:].bitcast(FP8X4), h_sc[:], hid[:].rearrange("p j t -> p (j t)"))
            nc.tensor.matmul_mx(
                prod[s][:],
                lhsT=h_codes[:].bitcast(FP8X4),
                lhsT_scale=h_sc[:],
                rhs=wb_sb[:].bitcast(FP4X4),
                rhs_scale=wb_sc[:],
                start=True,
                stop=True,
            )

        def peak(s):
            mag = ring.tile([P, N], F32, name="mag")
            nc.scalar.activation(mag[:], prod[s][:], ACT.Abs)
            den = ring.tile([P, 1], F32, name="den")
            nc.vector.tensor_scalar(mag[:], mag[:], 0.2, None, ALU.add, ALU.max, accum_out=den[:])
            return den

        def invert(den):
            inv = ring.tile([P, 1], F32, name="inv")
            nc.vector.reciprocal(inv[:], den[:])
            return inv

        def finish(s, inv):
            res = ring.tile([P, N], F32, name="res")
            nc.vector.scalar_tensor_tensor(res[:], prod[s][:], inv[:], rs3[:, s, :], ALU.mult, ALU.add)
            nc.sync.dma_start(out[s * P : (s + 1) * P, :], res[:])

        for s in range(SLICES):
            second_product(s)
        dens = [peak(s) for s in range(SLICES)]
        invs = [invert(den) for den in dens]
        for s in range(SLICES):
            finish(s, invs[s])
